import numpy as np, ml_dtypes
CORES = [8,136,40,168]
N = 4
import mx_ref
NC, WB = 256, 1
D = 2 * WB + 1
BF = ml_dtypes.bfloat16
def setup_inputs(rng):
    def f(*shape):
        return mx_ref.flush((rng.standard_normal(shape, dtype=np.float32) * np.exp2(rng.integers(-2, 3, shape[:-1] + (1,)))).astype(BF))
    return {"w": f(N, 128, D * 512), "x": f(N, 128, 4 * NC)}
def setup_inputs_blocks(rng):
    d = setup_inputs(rng)
    for k in ("w", "x"): d[k] = mx_ref.spread(d[k], rng, 1)
    return d
def setup_inputs_wide(rng):
    d = setup_inputs(rng)
    for k in ("w", "x"): d[k] = mx_ref.flush((d[k].astype(np.float32) * np.exp2(rng.integers(-8, 9, (N, 1, 1))).astype(np.float32)).astype(BF))
    return d
def setup_inputs_zeros(rng):
    d = setup_inputs(rng); v = d["x"].reshape(N, 128, -1, 4).copy()
    v[np.broadcast_to((rng.random((N, 1, v.shape[2], 1)) < 0.33), v.shape)] = 0
    d["x"] = v.reshape(d["x"].shape)
    return d
def reference(w, x):
    QX = [mx_ref.quantize(x[j]) for j in range(N)]
    y = np.zeros((N, 128, NC), np.float32)
    for r in range(N):
        for i in range(D):
            p = mx_ref.matmul(mx_ref.quantize(w[r][:, 512 * i:512 * i + 512]), QX[(r + i - WB) % N])
            y[r] = p if i == 0 else y[r] + p
    return {"y": y}

@@ -1,0 +1,101 @@
+from concourse.bass import DstId, RemoteDMATransfer
+from concourse.mybir import dt, ActivationFunctionType
+
+NCOL = 256
+HALF = NCOL // 2
+NW = 3
+BANK = 512
+
+SCRATCH = {
+    "xb": ("sbuf", [128, 4 * NCOL], "bfloat16"),
+    "wb": ("sbuf", [128, NW * 512], "bfloat16"),
+    "xq": ("sbuf", [128, NCOL], "float8_e4m3fn_x4"),
+    "xs": ("sbuf", [128, NCOL], "uint8"),
+    "lq": ("sbuf", [128, NCOL], "float8_e4m3fn_x4"),
+    "ls": ("sbuf", [128, NCOL], "uint8"),
+    "rq": ("sbuf", [128, NCOL], "float8_e4m3fn_x4"),
+    "rs": ("sbuf", [128, NCOL], "uint8"),
+    "wq": ("sbuf", [128, NW * 128], "float8_e4m3fn_x4"),
+    "ws": ("sbuf", [128, NW * 128], "uint8"),
+    "acc": ("psum", [128, 2 * BANK], "float32"),
+    "yb": ("sbuf", [128, NCOL], "float32"),
+}
+SEMAPHORES = ["sx", "sw", "qx", "qw", "arrl", "arrr", "sent", "m0", "m1", "c0", "c1", "st"]
+
+
+def _engines(mask):
+    return [e for e in range(16) if (mask >> e) & 1]
+
+
+def _mask_of(engines):
+    m = 0
+    for e in engines:
+        m |= 1 << e
+    return m
+
+
+def rank_program(g, core, T, topo):
+    rank = T.rank_of(core)
+    if rank is None:
+        return
+    S = T.sem
+    n = len(T.cores)
+    nxt = T.cores[(rank + 1) % n]
+    prv = T.cores[(rank - 1) % n]
+    assert topo.may_write(core, nxt) and topo.may_write(core, prv)
+
+    g.sync.dma_start(T.xb[:], T.x[:]).then_inc(S.sx, 16)
+    g.sync.dma_start(T.wb[:], T.w[:]).then_inc(S.sw, 16)
+
+    g.vector.wait_ge(S.sx, 16)
+    g.vector.quantize_mx(T.xq[:], T.xs[:], T.xb[:]).then_inc(S.qx, 1)
+    g.vector.wait_ge(S.sw, 16)
+    for i in range(NW):
+        g.vector.quantize_mx(T.wq[:, 128 * i:128 * i + 128], T.ws[:, 128 * i:128 * i + 128],
+                             T.wb[:, 512 * i:512 * i + 512]).then_inc(S.qw, 1)
+
+    rid_n, pid_n = topo.addr(nxt, core)
+    rid_p, pid_p = topo.addr(prv, core)
+    mask_n, mask_p = topo.mask(core, nxt), topo.mask(core, prv)
+    en, ep = _engines(mask_n), _engines(mask_p)
+    low, high = en[:len(en) // 2], ep[len(ep) // 2:]
+    assert not set(low) & set(high)
+    g.wait_ge(S.qx, 1)
+    g.remote_dma(T.lq[:].bitcast(dt.uint8), T.xq[:].bitcast(dt.uint8), S.arrl, S.sent, pid_n, rid_n, mask_n)
+    g.remote_dma_fused([
+        RemoteDMATransfer(dst_ids=[DstId(rid=rid_n, pnc=pid_n)], dma_engine_mask=_mask_of(low), remote_sem=S.arrl,
+                          src=T.xs[:], dst=T.ls[:]),
+        RemoteDMATransfer(dst_ids=[DstId(rid=rid_p, pnc=pid_p)], dma_engine_mask=_mask_of(high), remote_sem=S.arrr,
+                          src=T.xs[:], dst=T.rs[:]),
+    ], local_sem=S.sent)
+    g.remote_dma(T.rq[:].bitcast(dt.uint8), T.xq[:].bitcast(dt.uint8), S.arrr, S.sent, pid_p, rid_p, mask_p)
+    from_l = len(_engines(topo.mask(prv, core))) + len(_engines(topo.mask(prv, core))) // 2
+    from_r = len(_engines(topo.mask(nxt, core))) + len(_engines(topo.mask(nxt, core))) // 2
+
+    def mm(i, q, s, h, start, stop):
+        return g.tensor.matmul_mx(T.acc[:, BANK * h:BANK * h + HALF],
+                                  T.wq[:, 128 * i:128 * i + 128], T.ws[:, 128 * i:128 * i + 128],
+                                  q[:, HALF * h:HALF * h + HALF], s[:, HALF * h:HALF * h + HALF], start, stop)
+
+    g.tensor.wait_ge(S.qx, 1)
+    g.tensor.wait_ge(S.qw, NW)
+    mm(1, T.xq, T.xs, 0, True, False)
+    mm(1, T.xq, T.xs, 1, True, False)
+    g.tensor.wait_ge(S.arrl, from_l)
+    mm(0, T.lq, T.ls, 0, False, False)
+    mm(0, T.lq, T.ls, 1, False, False)
+    g.tensor.wait_ge(S.arrr, from_r)
+    mm(2, T.rq, T.rs, 0, False, True).then_inc(S.m0, 1)
+    mm(2, T.rq, T.rs, 1, False, True).then_inc(S.m1, 1)
+
+    g.vector.wait_ge(S.m0, 1)
+    g.vector.tensor_copy(T.yb[:, 0:HALF], T.acc[:, 0:HALF]).then_inc(S.c0, 1)
+    g.scalar.wait_ge(S.m1, 1)
+    g.scalar.activation(T.yb[:, HALF:NCOL], T.acc[:, BANK:BANK + HALF], ActivationFunctionType.Copy).then_inc(S.c1, 1)
+
+    g.sync.wait_ge(S.c0, 1)
+    g.sync.wait_ge(S.c1, 1)
+    g.sync.dma_start(T.y[:], T.yb[:]).then_inc(S.st, 16)
+    g.sync.wait_ge(S.st, 16)
+
+    g.wait_ge(S.sent, len(en) + len(low) + len(high) + len(ep))

@@ -20,7 +20,7 @@ SCRATCH = {
     "acc": ("psum", [128, 2 * BANK], "float32"),
     "yb": ("sbuf", [128, NCOL], "float32"),
 }
-SEMAPHORES = ["sx", "sw", "qx", "qw", "arrl", "arrr", "sent", "m0", "m1", "c0", "c1", "st"]
+SEMAPHORES = ["sx0", "sx1", "sw", "qx0", "qx1", "qw", "arrl", "arrr", "sent", "m0", "m1", "c0", "c1", "st"]
 
 
 def _engines(mask):
@@ -44,11 +44,14 @@ def rank_program(g, core, T, topo):
     prv = T.cores[(rank - 1) % n]
     assert topo.may_write(core, nxt) and topo.may_write(core, prv)
 
-    g.sync.dma_start(T.xb[:], T.x[:]).then_inc(S.sx, 16)
+    g.sync.dma_start(T.xb[:, 0:4 * HALF], T.x[:, 0:4 * HALF]).then_inc(S.sx0, 16)
+    g.sync.dma_start(T.xb[:, 4 * HALF:4 * NCOL], T.x[:, 4 * HALF:4 * NCOL]).then_inc(S.sx1, 16)
     g.sync.dma_start(T.wb[:], T.w[:]).then_inc(S.sw, 16)
 
-    g.vector.wait_ge(S.sx, 16)
-    g.vector.quantize_mx(T.xq[:], T.xs[:], T.xb[:]).then_inc(S.qx, 1)
+    g.vector.wait_ge(S.sx0, 16)
+    g.vector.quantize_mx(T.xq[:, 0:HALF], T.xs[:, 0:HALF], T.xb[:, 0:4 * HALF]).then_inc(S.qx0, 1)
+    g.vector.wait_ge(S.sx1, 16)
+    g.vector.quantize_mx(T.xq[:, HALF:NCOL], T.xs[:, HALF:NCOL], T.xb[:, 4 * HALF:4 * NCOL]).then_inc(S.qx1, 1)
     g.vector.wait_ge(S.sw, 16)
     for i in range(NW):
         g.vector.quantize_mx(T.wq[:, 128 * i:128 * i + 128], T.ws[:, 128 * i:128 * i + 128],
@@ -60,8 +63,11 @@ def rank_program(g, core, T, topo):
     en, ep = _engines(mask_n), _engines(mask_p)
     low, high = en[:len(en) // 2], ep[len(ep) // 2:]
     assert not set(low) & set(high)
-    g.wait_ge(S.qx, 1)
-    g.remote_dma(T.lq[:].bitcast(dt.uint8), T.xq[:].bitcast(dt.uint8), S.arrl, S.sent, pid_n, rid_n, mask_n)
+    g.wait_ge(S.qx0, 1)
+    g.remote_dma(T.lq[:, 0:HALF].bitcast(dt.uint8), T.xq[:, 0:HALF].bitcast(dt.uint8), S.arrl, S.sent, pid_n, rid_n, mask_n)
+    g.wait_ge(S.qx1, 1)
+    g.remote_dma(T.lq[:, HALF:NCOL].bitcast(dt.uint8), T.xq[:, HALF:NCOL].bitcast(dt.uint8), S.arrl, S.sent,
+                 pid_n, rid_n, mask_n)
     g.remote_dma_fused([
         RemoteDMATransfer(dst_ids=[DstId(rid=rid_n, pnc=pid_n)], dma_engine_mask=_mask_of(low), remote_sem=S.arrl,
                           src=T.xs[:], dst=T.ls[:]),
@@ -69,15 +75,17 @@ def rank_program(g, core, T, topo):
                           src=T.xs[:], dst=T.rs[:]),
     ], local_sem=S.sent)
     g.remote_dma(T.rq[:].bitcast(dt.uint8), T.xq[:].bitcast(dt.uint8), S.arrr, S.sent, pid_p, rid_p, mask_p)
-    from_l = len(_engines(topo.mask(prv, core))) + len(_engines(topo.mask(prv, core))) // 2
-    from_r = len(_engines(topo.mask(nxt, core))) + len(_engines(topo.mask(nxt, core))) // 2
+    el, er = len(_engines(topo.mask(prv, core))), len(_engines(topo.mask(nxt, core)))
+    from_l = 2 * el + el // 2
+    from_r = er + er // 2
 
     def mm(i, q, s, h, start, stop):
         return g.tensor.matmul_mx(T.acc[:, BANK * h:BANK * h + HALF],
                                   T.wq[:, 128 * i:128 * i + 128], T.ws[:, 128 * i:128 * i + 128],
                                   q[:, HALF * h:HALF * h + HALF], s[:, HALF * h:HALF * h + HALF], start, stop)
 
-    g.tensor.wait_ge(S.qx, 1)
+    g.tensor.wait_ge(S.qx0, 1)
+    g.tensor.wait_ge(S.qx1, 1)
     g.tensor.wait_ge(S.qw, NW)
     mm(1, T.xq, T.xs, 0, True, False)
     mm(1, T.xq, T.xs, 1, True, False)
@@ -98,4 +106,4 @@ def rank_program(g, core, T, topo):
     g.sync.dma_start(T.y[:], T.yb[:]).then_inc(S.st, 16)
     g.sync.wait_ge(S.st, 16)
 
-    g.wait_ge(S.sent, len(en) + len(low) + len(high) + len(ep))
+    g.wait_ge(S.sent, 2 * len(en) + len(low) + len(high) + len(ep))

from concourse.bass import DstId, RemoteDMATransfer
from concourse.mybir import dt, ActivationFunctionType

NCOL = 256
HALF = NCOL // 2
NW = 3
BANK = 512

SCRATCH = {
    "xb": ("sbuf", [128, 4 * NCOL], "bfloat16"),
    "wb": ("sbuf", [128, NW * 512], "bfloat16"),
    "xq": ("sbuf", [128, NCOL], "float8_e4m3fn_x4"),
    "xs": ("sbuf", [128, NCOL], "uint8"),
    "lq": ("sbuf", [128, NCOL], "float8_e4m3fn_x4"),
    "ls": ("sbuf", [128, NCOL], "uint8"),
    "rq": ("sbuf", [128, NCOL], "float8_e4m3fn_x4"),
    "rs": ("sbuf", [128, NCOL], "uint8"),
    "wq": ("sbuf", [128, NW * 128], "float8_e4m3fn_x4"),
    "ws": ("sbuf", [128, NW * 128], "uint8"),
    "acc": ("psum", [128, 2 * BANK], "float32"),
    "yb": ("sbuf", [128, NCOL], "float32"),
}
SEMAPHORES = ["sx0", "sx1", "sw", "qx0", "qx1", "qw", "arrl", "arrr", "sent", "m0", "m1", "c0", "c1", "st"]


def _engines(mask):
    return [e for e in range(16) if (mask >> e) & 1]


def _mask_of(engines):
    m = 0
    for e in engines:
        m |= 1 << e
    return m


def rank_program(g, core, T, topo):
    rank = T.rank_of(core)
    if rank is None:
        return
    S = T.sem
    n = len(T.cores)
    nxt = T.cores[(rank + 1) % n]
    prv = T.cores[(rank - 1) % n]
    assert topo.may_write(core, nxt) and topo.may_write(core, prv)

    g.sync.dma_start(T.xb[:, 0:4 * HALF], T.x[:, 0:4 * HALF]).then_inc(S.sx0, 16)
    g.sync.dma_start(T.xb[:, 4 * HALF:4 * NCOL], T.x[:, 4 * HALF:4 * NCOL]).then_inc(S.sx1, 16)
    g.sync.dma_start(T.wb[:], T.w[:]).then_inc(S.sw, 16)

    g.vector.wait_ge(S.sx0, 16)
    g.vector.quantize_mx(T.xq[:, 0:HALF], T.xs[:, 0:HALF], T.xb[:, 0:4 * HALF]).then_inc(S.qx0, 1)
    g.vector.wait_ge(S.sx1, 16)
    g.vector.quantize_mx(T.xq[:, HALF:NCOL], T.xs[:, HALF:NCOL], T.xb[:, 4 * HALF:4 * NCOL]).then_inc(S.qx1, 1)
    g.vector.wait_ge(S.sw, 16)
    for i in range(NW):
        g.vector.quantize_mx(T.wq[:, 128 * i:128 * i + 128], T.ws[:, 128 * i:128 * i + 128],
                             T.wb[:, 512 * i:512 * i + 512]).then_inc(S.qw, 1)

    rid_n, pid_n = topo.addr(nxt, core)
    rid_p, pid_p = topo.addr(prv, core)
    mask_n, mask_p = topo.mask(core, nxt), topo.mask(core, prv)
    en, ep = _engines(mask_n), _engines(mask_p)
    low, high = en[:len(en) // 2], ep[len(ep) // 2:]
    assert not set(low) & set(high)
    g.wait_ge(S.qx0, 1)
    g.remote_dma(T.lq[:, 0:HALF].bitcast(dt.uint8), T.xq[:, 0:HALF].bitcast(dt.uint8), S.arrl, S.sent, pid_n, rid_n, mask_n)
    g.wait_ge(S.qx1, 1)
    g.remote_dma(T.lq[:, HALF:NCOL].bitcast(dt.uint8), T.xq[:, HALF:NCOL].bitcast(dt.uint8), S.arrl, S.sent,
                 pid_n, rid_n, mask_n)
    g.remote_dma_fused([
        RemoteDMATransfer(dst_ids=[DstId(rid=rid_n, pnc=pid_n)], dma_engine_mask=_mask_of(low), remote_sem=S.arrl,
                          src=T.xs[:], dst=T.ls[:]),
        RemoteDMATransfer(dst_ids=[DstId(rid=rid_p, pnc=pid_p)], dma_engine_mask=_mask_of(high), remote_sem=S.arrr,
                          src=T.xs[:], dst=T.rs[:]),
    ], local_sem=S.sent)
    g.remote_dma(T.rq[:].bitcast(dt.uint8), T.xq[:].bitcast(dt.uint8), S.arrr, S.sent, pid_p, rid_p, mask_p)
    el, er = len(_engines(topo.mask(prv, core))), len(_engines(topo.mask(nxt, core)))
    from_l = 2 * el + el // 2
    from_r = er + er // 2

    def mm(i, q, s, h, start, stop):
        return g.tensor.matmul_mx(T.acc[:, BANK * h:BANK * h + HALF],
                                  T.wq[:, 128 * i:128 * i + 128], T.ws[:, 128 * i:128 * i + 128],
                                  q[:, HALF * h:HALF * h + HALF], s[:, HALF * h:HALF * h + HALF], start, stop)

    g.tensor.wait_ge(S.qx0, 1)
    g.tensor.wait_ge(S.qx1, 1)
    g.tensor.wait_ge(S.qw, NW)
    mm(1, T.xq, T.xs, 0, True, False)
    mm(1, T.xq, T.xs, 1, True, False)
    g.tensor.wait_ge(S.arrl, from_l)
    mm(0, T.lq, T.ls, 0, False, False)
    mm(0, T.lq, T.ls, 1, False, False)
    g.tensor.wait_ge(S.arrr, from_r)
    mm(2, T.rq, T.rs, 0, False, True).then_inc(S.m0, 1)
    mm(2, T.rq, T.rs, 1, False, True).then_inc(S.m1, 1)

    g.vector.wait_ge(S.m0, 1)
    g.vector.tensor_copy(T.yb[:, 0:HALF], T.acc[:, 0:HALF]).then_inc(S.c0, 1)
    g.scalar.wait_ge(S.m1, 1)
    g.scalar.activation(T.yb[:, HALF:NCOL], T.acc[:, BANK:BANK + HALF], ActivationFunctionType.Copy).then_inc(S.c1, 1)

    g.sync.wait_ge(S.c0, 1)
    g.sync.wait_ge(S.c1, 1)
    g.sync.dma_start(T.y[:], T.yb[:]).then_inc(S.st, 16)
    g.sync.wait_ge(S.st, 16)

    g.wait_ge(S.sent, 2 * len(en) + len(low) + len(high) + len(ep))
